import numpy as np
import ml_dtypes


def mxq(x, axis, fmt="e4m3"):
    dtype, down = {"e4m3": (ml_dtypes.float8_e4m3fn, 7), "e5m2": (ml_dtypes.float8_e5m2, 14)}[fmt]
    v = np.moveaxis(np.asarray(x, np.float32).astype(ml_dtypes.bfloat16).astype(np.float64), axis, -1)
    blocks = v.reshape(v.shape[:-1] + (-1, 32))
    amax = np.abs(blocks).max(-1, keepdims=True)
    byte = np.maximum(np.where(amax > 0, np.frexp(amax)[1] - 1 + 127, 0) - down, 1)
    scale = np.exp2(byte - 127.0)
    codes = (blocks / scale).astype(np.float32).astype(dtype).astype(np.float64)
    return np.moveaxis((codes * scale).reshape(v.shape), -1, axis)


WIDE = False


def mx_kscale(k):
    if not WIDE:
        return np.ones(k)
    levels = np.array([10, -10, 5, -5, 0])
    if k % 512:
        return np.exp2(np.random.permutation(np.resize(levels, k // 32))).repeat(32)
    a = np.empty((k // 512, 16))
    for p in range(k // 512):
        a[p, :8] = np.random.permutation(np.resize(levels, 8))
        for g in range(8):
            far = levels[np.abs(levels - a[p, g]) >= 10]
            a[p, g + 8] = far[np.random.randint(len(far))]
    return np.exp2(a.ravel()).repeat(32)


def f64(x):
    return np.asarray(x).astype(np.float64)


def striped(idx):
    return np.tile(idx.reshape(-1, 16).T, (8, 1)).astype(np.uint16)


def unstriped(offs):
    return offs[:16].T.reshape(-1).astype(np.int64)


def pack_weight(w):
    k, n = w.shape
    w = f64(np.asarray(w, np.float32).astype(ml_dtypes.bfloat16)).reshape(k // 32, 32, n)
    amax = np.abs(w).max(1)
    byte = np.clip(np.where(amax > 0, np.frexp(amax)[1] - 1 + 127 - 7, 1), 1, 254)
    scaled = (w * np.exp2(127.0 - byte)[:, None, :]).reshape(k, n).astype(np.float32)
    words = np.ascontiguousarray(scaled.reshape(k // 512, 128, 4, n).transpose(0, 1, 3, 2)).astype(ml_dtypes.float8_e4m3fn).view(np.uint8)
    return words, np.ascontiguousarray(byte.astype(np.uint8).reshape(k // 512, 16, n))


def unpack_weight(words, scales):
    g, p, n, _ = words.shape
    vals = np.ascontiguousarray(words).view(ml_dtypes.float8_e4m3fn).astype(np.float64) * np.repeat(np.exp2(scales.astype(np.float64) - 127.0), 8, axis=1)[..., None]
    return vals.transpose(0, 1, 3, 2).reshape(g * 512, n)


def relu(v):
    return np.maximum(v, 0.0)


K, T, S, N, W = 512, 1024, 512, 128, 2048


def setup_inputs():
    n = np.random.standard_normal
    s = mx_kscale(K)[:, None]
    packed_xT = pack_weight(n((K, T)) * s)
    packed_eT = pack_weight(n((K, W)) * s)
    return {
        "x_words": packed_xT[0],
        "x_scales": packed_xT[1],
        "e_words": packed_eT[0],
        "e_scales": packed_eT[1],
        "wo0": (n((K, N)) / np.sqrt(K) / s).astype(np.float32),
        "wf0": (n((K, N)) / np.sqrt(K) / s).astype(np.float32),
        "wo1": (n((K, N)) / np.sqrt(K) / s).astype(np.float32),
        "wf1": (n((K, N)) / np.sqrt(K) / s).astype(np.float32),
        "offs": striped(np.random.permutation(T)[:S]),
        "radar": striped(np.random.permutation(W)[:S]),
    }


def reference(x_words, x_scales, e_words, e_scales, wo0, wf0, wo1, wf1, offs, radar):
    xq = unpack_weight(x_words, x_scales)[:, unstriped(offs)]
    eo0 = relu(mxq(f64(wo0), 0, "e4m3").T @ xq)
    ef0 = relu(mxq(f64(wf0), 0, "e4m3").T @ xq)
    t0 = eo0 + ef0 + 2.0
    mo0 = eo0 / t0
    e_radar = unpack_weight(e_words, e_scales)[:, unstriped(radar)]
    eo1 = relu(mxq(f64(wo1), 0, "e4m3").T @ e_radar)
    ef1 = relu(mxq(f64(wf1), 0, "e4m3").T @ e_radar)
    t1 = eo1 + ef1 + 2.0
    mo1 = eo1 / t1
    mf1 = ef1 / t1
    nu = -1.0 * (mo1 + mf1) + 1.0
    mf0 = ef0 / t0
    mu = -1.0 * (mo0 + mf0) + 1.0
    agree = -1.0 * (mo0 * mf1 + mf0 * mo1) + 1.0
    oc = (mo0 * mo1 + mo0 * nu + mu * mo1) / agree
    return oc - ((mf0 * mf1 + mf0 * nu + mu * mf1) / agree)

@@ -1,0 +1,141 @@
+from contextlib import ExitStack
+
+import concourse.mybir as mybir
+
+K, T, S, N, W = 512, 1024, 512, 128, 2048
+FLOPS = 4 * 2 * K * N * S
+
+F32 = mybir.dt.float32
+BF16 = mybir.dt.bfloat16
+I32 = mybir.dt.int32
+U32 = mybir.dt.uint32
+U16 = mybir.dt.uint16
+U8 = mybir.dt.uint8
+FP8X4 = mybir.dt.float8_e4m3fn_x4
+ALU = mybir.AluOpType
+ACT = mybir.ActivationFunctionType
+
+P = 128
+H = 256
+HALVES = S // H
+
+
+def tile_picked_yds_diff_p_kernel(
+    tc, x_words, x_scales, e_words, e_scales, wo0, wf0, wo1, wf1, offs, radar, out
+):
+    nc = tc.nc
+    with ExitStack() as ctx:
+        sb = ctx.enter_context(tc.tile_pool(name="sb", bufs=1))
+        ps = ctx.enter_context(tc.psum_pool(name="ps", bufs=1))
+
+        offs_t = sb.tile([P, S // 16], U16, name="offs_t")
+        radar_t = sb.tile([P, S // 16], U16, name="radar_t")
+        xw = sb.tile([P, T], U32, name="xw")
+        ew = sb.tile([P, W], U32, name="ew")
+        xs = sb.tile([P, T], U8, name="xs")
+        es = sb.tile([P, W], U8, name="es")
+        warm_in = sb.tile([P, 1], F32, name="warm_in")
+        warm_out = sb.tile([P, 1], F32, name="warm_out")
+
+        nc.vector.memset(xs[:].bitcast(I32), 0)
+        nc.vector.memset(es[:].bitcast(I32), 0)
+        nc.vector.memset(warm_in[:], 1.0)
+
+        def load_scales(eng, tile, src):
+            for q in range(4):
+                eng.dma_start(tile[32 * q : 32 * q + 4, :].bitcast(I32), src[0, 4 * q : 4 * q + 4, :].bitcast(I32))
+
+        def load_words(tile, src):
+            nc.sync.dma_start(tile[:].bitcast(I32), src[0].rearrange("p n t -> p (n t)").bitcast(I32))
+
+        raw = {}
+
+        def load_weight(name, src):
+            raw[name] = sb.tile([P, 4, N], F32, name="raw_" + name)
+            nc.sync.dma_start(raw[name][:], src.rearrange("(p j) c -> p j c", j=4))
+
+        nc.sync.dma_start(offs_t[:], offs)
+        load_scales(nc.sync, xs, x_scales)
+        nc.scalar.activation(warm_out[:], warm_in[:], ACT.Abs_reciprocal_sqrt)
+        load_words(xw, x_words)
+        load_weight("wo0", wo0)
+        load_weight("wf0", wf0)
+        nc.sync.dma_start(radar_t[:], radar)
+        load_weight("wo1", wo1)
+        load_words(ew, e_words)
+        load_weight("wf1", wf1)
+        load_scales(nc.scalar, es, e_scales)
+
+        codes = {}
+        scales = {}
+
+        def quantise(name):
+            grouped = sb.tile([P, N, 4], BF16, name="grp_" + name, align_bytes=64)
+            nc.scalar.copy(grouped[:], raw[name][:].rearrange("p j c -> p c j"))
+            codes[name] = sb.tile([P, N], U32, name="codes_" + name, align_bytes=64)
+            scales[name] = sb.tile([P, N], U8, name="scales_" + name, align_bytes=64)
+            nc.vector.quantize_mx(
+                out=codes[name][:].bitcast(FP8X4), scales=scales[name][:], in_=grouped[:].rearrange("p c j -> p (c j)")
+            )
+
+        def product(bank, name, words, plane):
+            nc.tensor.matmul_mx(
+                out=bank,
+                lhsT=codes[name][:].bitcast(FP8X4),
+                lhsT_scale=scales[name][:],
+                rhs=words.bitcast(FP8X4),
+                rhs_scale=plane,
+                start=True,
+                stop=True,
+            )
+
+        gxs = sb.tile([P, S], U8, name="gxs", align_bytes=64)
+        gxw = sb.tile([P, S], U32, name="gxw", align_bytes=64)
+        ges = sb.tile([P, S], U8, name="ges", align_bytes=64)
+        nc.vector.tensor_copy(gxs[:], xs[:].indirect(offs_t[:]))
+        nc.vector.tensor_copy(gxw[:], xw[:].indirect(offs_t[:]))
+        quantise("wo0")
+        quantise("wf0")
+        nc.vector.tensor_copy(ges[:], es[:].indirect(radar_t[:]))
+        quantise("wo1")
+
+        plus2 = {}
+        for name in ("wo0", "wf0"):
+            bank = ps.tile([P, S], F32, name="ps_" + name)
+            product(bank[:], name, gxw[:], gxs[:])
+            rect = sb.tile([P, S], F32, name="rect_" + name)
+            nc.scalar.activation(rect[:], bank[:], ACT.Relu)
+            plus2[name] = sb.tile([P, S], F32, name="plus2_" + name)
+            nc.scalar.activation(plus2[name][:], rect[:], ACT.Identity, bias=2.0)
+
+        gew = []
+        for h in range(HALVES):
+            g = sb.tile([P, H], U32, name="gew%d" % h, align_bytes=64)
+            nc.vector.tensor_copy(g[:], ew[:].indirect(radar_t[:, h * H // 16 : (h + 1) * H // 16]))
+            gew.append(g)
+        quantise("wf1")
+
+        prod = {}
+        for name, other in (("wo1", "wo0"), ("wf1", "wf0")):
+            for h in range(HALVES):
+                cols = slice(h * H, (h + 1) * H)
+                bank = ps.tile([P, H], F32, name="ps_%s_%d" % (name, h))
+                product(bank[:], name, gew[h][:], ges[:, cols])
+                rect = sb.tile([P, H], F32, name="rect_%s_%d" % (name, h))
+                nc.scalar.activation(rect[:], bank[:], ACT.Relu)
+                prod[name, h] = sb.tile([P, H], F32, name="prod_%s_%d" % (name, h))
+                nc.vector.scalar_tensor_tensor(prod[name, h][:], rect[:], 2.0, plus2[other][:, cols], ALU.add, ALU.mult)
+
+        for h in range(HALVES):
+            cols = slice(h * H, (h + 1) * H)
+            den = sb.tile([P, H], F32, name="den%d" % h)
+            nc.vector.tensor_tensor(den[:], prod["wo1", h][:], prod["wf1", h][:], ALU.add)
+            root = sb.tile([P, H], F32, name="root%d" % h)
+            nc.scalar.activation(root[:], den[:], ACT.Abs_reciprocal_sqrt, bias=-4.0)
+            inv = sb.tile([P, H], F32, name="inv%d" % h)
+            nc.scalar.activation(inv[:], root[:], ACT.Square)
+            num = sb.tile([P, H], F32, name="num%d" % h)
+            nc.vector.tensor_tensor(num[:], prod["wo1", h][:], prod["wf1", h][:], ALU.subtract)
+            res = sb.tile([P, H], F32, name="res%d" % h)
+            nc.vector.tensor_tensor(res[:], num[:], inv[:], ALU.mult)
+            nc.sync.dma_start(out[:, cols], res[:])

@@ -17,7 +17,7 @@ ACT = mybir.ActivationFunctionType
 
 P = 128
 H = 256
-HALVES = S // H
+CHUNKS = ((0, 128), (128, 128), (256, 128), (384, 128))
 
 
 def tile_picked_yds_diff_p_kernel(
@@ -26,23 +26,25 @@ def tile_picked_yds_diff_p_kernel(
     nc = tc.nc
     with ExitStack() as ctx:
         sb = ctx.enter_context(tc.tile_pool(name="sb", bufs=1))
+        reuse = ctx.enter_context(tc.tile_pool(name="reuse", bufs=1))
         ps = ctx.enter_context(tc.psum_pool(name="ps", bufs=1))
 
         offs_t = sb.tile([P, S // 16], U16, name="offs_t")
         radar_t = sb.tile([P, S // 16], U16, name="radar_t")
         xw = sb.tile([P, T], U32, name="xw")
         ew = sb.tile([P, W], U32, name="ew")
-        xs = sb.tile([P, T], U8, name="xs")
-        es = sb.tile([P, W], U8, name="es")
+        xs = reuse.tile([P, T], U8, name="xs", offset=0, align_bytes=64)
+        es = reuse.tile([P, W], U8, name="es", offset=T, align_bytes=64)
         warm_in = sb.tile([P, 1], F32, name="warm_in")
         warm_out = sb.tile([P, 1], F32, name="warm_out")
 
+        nc.vector.memset(warm_in[:], 1.0)
+        nc.scalar.activation(warm_out[:], warm_in[:], ACT.Abs_reciprocal_sqrt)
         nc.vector.memset(xs[:].bitcast(I32), 0)
         nc.vector.memset(es[:].bitcast(I32), 0)
-        nc.vector.memset(warm_in[:], 1.0)
 
-        def load_scales(eng, tile, src):
-            for q in range(4):
+        def load_scales(eng, tile, src, quads):
+            for q in quads:
                 eng.dma_start(tile[32 * q : 32 * q + 4, :].bitcast(I32), src[0, 4 * q : 4 * q + 4, :].bitcast(I32))
 
         def load_words(tile, src):
@@ -55,34 +57,35 @@ def tile_picked_yds_diff_p_kernel(
             nc.sync.dma_start(raw[name][:], src.rearrange("(p j) c -> p j c", j=4))
 
         nc.sync.dma_start(offs_t[:], offs)
-        load_scales(nc.sync, xs, x_scales)
-        nc.scalar.activation(warm_out[:], warm_in[:], ACT.Abs_reciprocal_sqrt)
+        nc.sync.dma_start(radar_t[:], radar)
+        load_scales(nc.gpsimd, xs, x_scales, (0, 1))
+        load_scales(nc.scalar, xs, x_scales, (2, 3))
+        load_scales(nc.gpsimd, es, e_scales, (0, 1))
         load_words(xw, x_words)
         load_weight("wo0", wo0)
         load_weight("wf0", wf0)
-        nc.sync.dma_start(radar_t[:], radar)
         load_weight("wo1", wo1)
-        load_words(ew, e_words)
         load_weight("wf1", wf1)
-        load_scales(nc.scalar, es, e_scales)
+        load_words(ew, e_words)
+        load_scales(nc.scalar, es, e_scales, (2, 3))
 
-        codes = {}
-        scales = {}
-
-        def quantise(name):
-            grouped = sb.tile([P, N, 4], BF16, name="grp_" + name, align_bytes=64)
-            nc.scalar.copy(grouped[:], raw[name][:].rearrange("p j c -> p c j"))
-            codes[name] = sb.tile([P, N], U32, name="codes_" + name, align_bytes=64)
-            scales[name] = sb.tile([P, N], U8, name="scales_" + name, align_bytes=64)
+        def quantise(names, offset):
+            grouped = sb.tile([P, 2, N, 4], BF16, name="grp_" + names[0], align_bytes=64)
+            for i, name in enumerate(names):
+                nc.scalar.copy(grouped[:, i], raw[name][:].rearrange("p j c -> p c j"))
+            codes = reuse.tile([P, 2 * N], U32, name="codes_" + names[0], offset=offset, align_bytes=64)
+            scales = sb.tile([P, 2 * N], U8, name="scales_" + names[0], align_bytes=64)
             nc.vector.quantize_mx(
-                out=codes[name][:].bitcast(FP8X4), scales=scales[name][:], in_=grouped[:].rearrange("p c j -> p (c j)")
+                out=codes[:].bitcast(FP8X4), scales=scales[:], in_=grouped[:].rearrange("p i c j -> p (i c j)")
             )
+            return codes, scales
 
-        def product(bank, name, words, plane):
+        def product(bank, weights, i, words, plane):
+            codes, scales = weights
             nc.tensor.matmul_mx(
                 out=bank,
-                lhsT=codes[name][:].bitcast(FP8X4),
-                lhsT_scale=scales[name][:],
+                lhsT=codes[:, i * N : (i + 1) * N].bitcast(FP8X4),
+                lhsT_scale=scales[:, i * N : (i + 1) * N],
                 rhs=words.bitcast(FP8X4),
                 rhs_scale=plane,
                 start=True,
@@ -92,50 +95,49 @@ def tile_picked_yds_diff_p_kernel(
         gxs = sb.tile([P, S], U8, name="gxs", align_bytes=64)
         gxw = sb.tile([P, S], U32, name="gxw", align_bytes=64)
         ges = sb.tile([P, S], U8, name="ges", align_bytes=64)
-        nc.vector.tensor_copy(gxs[:], xs[:].indirect(offs_t[:]))
         nc.vector.tensor_copy(gxw[:], xw[:].indirect(offs_t[:]))
-        quantise("wo0")
-        quantise("wf0")
+        nc.vector.tensor_copy(gxs[:], xs[:].indirect(offs_t[:]))
+        w0 = quantise(("wo0", "wf0"), 0)
         nc.vector.tensor_copy(ges[:], es[:].indirect(radar_t[:]))
-        quantise("wo1")
+        w1 = quantise(("wo1", "wf1"), T + 4 * H)
 
-        plus2 = {}
-        for name in ("wo0", "wf0"):
-            bank = ps.tile([P, S], F32, name="ps_" + name)
-            product(bank[:], name, gxw[:], gxs[:])
-            rect = sb.tile([P, S], F32, name="rect_" + name)
+        plus2 = sb.tile([P, 2, S], F32, name="plus2")
+        for i in range(2):
+            bank = ps.tile([P, S], F32, name="ps_x%d" % i)
+            product(bank[:], w0, i, gxw[:], gxs[:])
+            rect = sb.tile([P, S], F32, name="rect_x%d" % i)
             nc.scalar.activation(rect[:], bank[:], ACT.Relu)
-            plus2[name] = sb.tile([P, S], F32, name="plus2_" + name)
-            nc.scalar.activation(plus2[name][:], rect[:], ACT.Identity, bias=2.0)
+            nc.scalar.activation(plus2[:, i, :], rect[:], ACT.Identity, bias=2.0)
 
-        gew = []
-        for h in range(HALVES):
-            g = sb.tile([P, H], U32, name="gew%d" % h, align_bytes=64)
-            nc.vector.tensor_copy(g[:], ew[:].indirect(radar_t[:, h * H // 16 : (h + 1) * H // 16]))
-            gew.append(g)
-        quantise("wf1")
+        gew = [
+            reuse.tile([P, H], U32, name="gew0", offset=T, align_bytes=64),
+            sb.tile([P, H], U32, name="gew1", align_bytes=64),
+        ]
+        for h in range(S // H):
+            nc.vector.tensor_copy(gew[h][:], ew[:].indirect(radar_t[:, h * H // 16 : (h + 1) * H // 16]))
 
-        prod = {}
-        for name, other in (("wo1", "wo0"), ("wf1", "wf0")):
-            for h in range(HALVES):
-                cols = slice(h * H, (h + 1) * H)
-                bank = ps.tile([P, H], F32, name="ps_%s_%d" % (name, h))
-                product(bank[:], name, gew[h][:], ges[:, cols])
-                rect = sb.tile([P, H], F32, name="rect_%s_%d" % (name, h))
-                nc.scalar.activation(rect[:], bank[:], ACT.Relu)
-                prod[name, h] = sb.tile([P, H], F32, name="prod_%s_%d" % (name, h))
-                nc.vector.scalar_tensor_tensor(prod[name, h][:], rect[:], 2.0, plus2[other][:, cols], ALU.add, ALU.mult)
-
-        for h in range(HALVES):
-            cols = slice(h * H, (h + 1) * H)
-            den = sb.tile([P, H], F32, name="den%d" % h)
-            nc.vector.tensor_tensor(den[:], prod["wo1", h][:], prod["wf1", h][:], ALU.add)
-            root = sb.tile([P, H], F32, name="root%d" % h)
+        for c0, w in CHUNKS:
+            cols = slice(c0, c0 + w)
+            bank = ps.tile([P, 2, w], F32, name="ps_e%d" % c0)
+            for i in range(2):
+                product(bank[:, i, :], w1, i, gew[c0 // H][:, c0 % H : c0 % H + w], ges[:, cols])
+            rect = sb.tile([P, 2, w], F32, name="rect_e%d" % c0)
+            nc.scalar.activation(rect[:], bank[:], ACT.Relu)
+            prod = sb.tile([P, 2, w], F32, name="prod%d" % c0)
+            nc.vector.scalar_tensor_tensor(prod[:], rect[:], 2.0, plus2[:, :, cols], ALU.add, ALU.mult)
+            den = sb.tile([P, w], F32, name="den%d" % c0)
+            nc.vector.tensor_tensor(den[:], prod[:, 0, :], prod[:, 1, :], ALU.add)
+            root = sb.tile([P, w], F32, name="root%d" % c0)
             nc.scalar.activation(root[:], den[:], ACT.Abs_reciprocal_sqrt, bias=-4.0)
-            inv = sb.tile([P, H], F32, name="inv%d" % h)
+            inv = sb.tile([P, w], F32, name="inv%d" % c0)
             nc.scalar.activation(inv[:], root[:], ACT.Square)
-            num = sb.tile([P, H], F32, name="num%d" % h)
-            nc.vector.tensor_tensor(num[:], prod["wo1", h][:], prod["wf1", h][:], ALU.subtract)
-            res = sb.tile([P, H], F32, name="res%d" % h)
-            nc.vector.tensor_tensor(res[:], num[:], inv[:], ALU.mult)
+            res = sb.tile([P, w], F32, name="res%d" % c0)
+            if c0 < 256:
+                share = sb.tile([P, w], F32, name="share%d" % c0)
+                nc.vector.scalar_tensor_tensor(share[:], prod[:, 1, :], -2.0, inv[:], ALU.add, ALU.mult)
+                nc.scalar.activation(res[:], share[:], ACT.Identity, bias=1.0, scale=-2.0)
+            else:
+                num = sb.tile([P, w], F32, name="num%d" % c0)
+                nc.vector.tensor_tensor(num[:], prod[:, 0, :], prod[:, 1, :], ALU.subtract)
+                nc.vector.tensor_tensor(res[:], num[:], inv[:], ALU.mult)
             nc.sync.dma_start(out[:, cols], res[:])

@@ -33,14 +33,14 @@ def tile_picked_yds_diff_p_kernel(
         radar_t = sb.tile([P, S // 16], U16, name="radar_t")
         xw = sb.tile([P, T], U32, name="xw")
         ew = sb.tile([P, W], U32, name="ew")
-        xs = reuse.tile([P, T], U8, name="xs", offset=0, align_bytes=64)
-        es = reuse.tile([P, W], U8, name="es", offset=T, align_bytes=64)
+        xs = sb.tile([P, T], U8, name="xs")
+        es = reuse.tile([P, W], U8, name="es", offset=0, align_bytes=64)
         warm_in = sb.tile([P, 1], F32, name="warm_in")
         warm_out = sb.tile([P, 1], F32, name="warm_out")
 
+        nc.vector.memset(xs[:].bitcast(I32), 0)
         nc.vector.memset(warm_in[:], 1.0)
         nc.scalar.activation(warm_out[:], warm_in[:], ACT.Abs_reciprocal_sqrt)
-        nc.vector.memset(xs[:].bitcast(I32), 0)
         nc.vector.memset(es[:].bitcast(I32), 0)
 
         def load_scales(eng, tile, src, quads):
@@ -58,22 +58,20 @@ def tile_picked_yds_diff_p_kernel(
 
         nc.sync.dma_start(offs_t[:], offs)
         nc.sync.dma_start(radar_t[:], radar)
-        load_scales(nc.gpsimd, xs, x_scales, (0, 1))
-        load_scales(nc.scalar, xs, x_scales, (2, 3))
-        load_scales(nc.gpsimd, es, e_scales, (0, 1))
-        load_words(xw, x_words)
         load_weight("wo0", wo0)
+        load_scales(nc.sync, xs, x_scales, range(4))
+        load_words(xw, x_words)
         load_weight("wf0", wf0)
         load_weight("wo1", wo1)
         load_weight("wf1", wf1)
+        load_scales(nc.sync, es, e_scales, range(4))
         load_words(ew, e_words)
-        load_scales(nc.scalar, es, e_scales, (2, 3))
 
-        def quantise(names, offset):
+        def quantise(names, pool, **where):
             grouped = sb.tile([P, 2, N, 4], BF16, name="grp_" + names[0], align_bytes=64)
             for i, name in enumerate(names):
                 nc.scalar.copy(grouped[:, i], raw[name][:].rearrange("p j c -> p c j"))
-            codes = reuse.tile([P, 2 * N], U32, name="codes_" + names[0], offset=offset, align_bytes=64)
+            codes = pool.tile([P, 2 * N], U32, name="codes_" + names[0], align_bytes=64, **where)
             scales = sb.tile([P, 2 * N], U8, name="scales_" + names[0], align_bytes=64)
             nc.vector.quantize_mx(
                 out=codes[:].bitcast(FP8X4), scales=scales[:], in_=grouped[:].rearrange("p i c j -> p (i c j)")
@@ -97,9 +95,9 @@ def tile_picked_yds_diff_p_kernel(
         ges = sb.tile([P, S], U8, name="ges", align_bytes=64)
         nc.vector.tensor_copy(gxw[:], xw[:].indirect(offs_t[:]))
         nc.vector.tensor_copy(gxs[:], xs[:].indirect(offs_t[:]))
-        w0 = quantise(("wo0", "wf0"), 0)
+        w0 = quantise(("wo0", "wf0"), sb)
         nc.vector.tensor_copy(ges[:], es[:].indirect(radar_t[:]))
-        w1 = quantise(("wo1", "wf1"), T + 4 * H)
+        w1 = quantise(("wo1", "wf1"), reuse, offset=0)
 
         plus2 = sb.tile([P, 2, S], F32, name="plus2")
         for i in range(2):
@@ -110,7 +108,7 @@ def tile_picked_yds_diff_p_kernel(
             nc.scalar.activation(plus2[:, i, :], rect[:], ACT.Identity, bias=2.0)
 
         gew = [
-            reuse.tile([P, H], U32, name="gew0", offset=T, align_bytes=64),
+            sb.tile([P, H], U32, name="gew0", align_bytes=64),
             sb.tile([P, H], U32, name="gew1", align_bytes=64),
         ]
         for h in range(S // H):

from contextlib import ExitStack

import concourse.mybir as mybir

K, T, S, N, W = 512, 1024, 512, 128, 2048
FLOPS = 4 * 2 * K * N * S

F32 = mybir.dt.float32
BF16 = mybir.dt.bfloat16
I32 = mybir.dt.int32
U32 = mybir.dt.uint32
U16 = mybir.dt.uint16
U8 = mybir.dt.uint8
FP8X4 = mybir.dt.float8_e4m3fn_x4
ALU = mybir.AluOpType
ACT = mybir.ActivationFunctionType

P = 128
H = 256
CHUNKS = ((0, 128), (128, 128), (256, 128), (384, 128))


def tile_picked_yds_diff_p_kernel(
    tc, x_words, x_scales, e_words, e_scales, wo0, wf0, wo1, wf1, offs, radar, out
):
    nc = tc.nc
    with ExitStack() as ctx:
        sb = ctx.enter_context(tc.tile_pool(name="sb", bufs=1))
        reuse = ctx.enter_context(tc.tile_pool(name="reuse", bufs=1))
        ps = ctx.enter_context(tc.psum_pool(name="ps", bufs=1))

        offs_t = sb.tile([P, S // 16], U16, name="offs_t")
        radar_t = sb.tile([P, S // 16], U16, name="radar_t")
        xw = sb.tile([P, T], U32, name="xw")
        ew = sb.tile([P, W], U32, name="ew")
        xs = sb.tile([P, T], U8, name="xs")
        es = reuse.tile([P, W], U8, name="es", offset=0, align_bytes=64)
        warm_in = sb.tile([P, 1], F32, name="warm_in")
        warm_out = sb.tile([P, 1], F32, name="warm_out")

        nc.vector.memset(xs[:].bitcast(I32), 0)
        nc.vector.memset(warm_in[:], 1.0)
        nc.scalar.activation(warm_out[:], warm_in[:], ACT.Abs_reciprocal_sqrt)
        nc.vector.memset(es[:].bitcast(I32), 0)

        def load_scales(eng, tile, src, quads):
            for q in quads:
                eng.dma_start(tile[32 * q : 32 * q + 4, :].bitcast(I32), src[0, 4 * q : 4 * q + 4, :].bitcast(I32))

        def load_words(tile, src):
            nc.sync.dma_start(tile[:].bitcast(I32), src[0].rearrange("p n t -> p (n t)").bitcast(I32))

        raw = {}

        def load_weight(name, src):
            raw[name] = sb.tile([P, 4, N], F32, name="raw_" + name)
            nc.sync.dma_start(raw[name][:], src.rearrange("(p j) c -> p j c", j=4))

        nc.sync.dma_start(offs_t[:], offs)
        nc.sync.dma_start(radar_t[:], radar)
        load_weight("wo0", wo0)
        load_scales(nc.sync, xs, x_scales, range(4))
        load_words(xw, x_words)
        load_weight("wf0", wf0)
        load_weight("wo1", wo1)
        load_weight("wf1", wf1)
        load_scales(nc.sync, es, e_scales, range(4))
        load_words(ew, e_words)

        def quantise(names, pool, **where):
            grouped = sb.tile([P, 2, N, 4], BF16, name="grp_" + names[0], align_bytes=64)
            for i, name in enumerate(names):
                nc.scalar.copy(grouped[:, i], raw[name][:].rearrange("p j c -> p c j"))
            codes = pool.tile([P, 2 * N], U32, name="codes_" + names[0], align_bytes=64, **where)
            scales = sb.tile([P, 2 * N], U8, name="scales_" + names[0], align_bytes=64)
            nc.vector.quantize_mx(
                out=codes[:].bitcast(FP8X4), scales=scales[:], in_=grouped[:].rearrange("p i c j -> p (i c j)")
            )
            return codes, scales

        def product(bank, weights, i, words, plane):
            codes, scales = weights
            nc.tensor.matmul_mx(
                out=bank,
                lhsT=codes[:, i * N : (i + 1) * N].bitcast(FP8X4),
                lhsT_scale=scales[:, i * N : (i + 1) * N],
                rhs=words.bitcast(FP8X4),
                rhs_scale=plane,
                start=True,
                stop=True,
            )

        gxs = sb.tile([P, S], U8, name="gxs", align_bytes=64)
        gxw = sb.tile([P, S], U32, name="gxw", align_bytes=64)
        ges = sb.tile([P, S], U8, name="ges", align_bytes=64)
        nc.vector.tensor_copy(gxw[:], xw[:].indirect(offs_t[:]))
        nc.vector.tensor_copy(gxs[:], xs[:].indirect(offs_t[:]))
        w0 = quantise(("wo0", "wf0"), sb)
        nc.vector.tensor_copy(ges[:], es[:].indirect(radar_t[:]))
        w1 = quantise(("wo1", "wf1"), reuse, offset=0)

        plus2 = sb.tile([P, 2, S], F32, name="plus2")
        for i in range(2):
            bank = ps.tile([P, S], F32, name="ps_x%d" % i)
            product(bank[:], w0, i, gxw[:], gxs[:])
            rect = sb.tile([P, S], F32, name="rect_x%d" % i)
            nc.scalar.activation(rect[:], bank[:], ACT.Relu)
            nc.scalar.activation(plus2[:, i, :], rect[:], ACT.Identity, bias=2.0)

        gew = [
            sb.tile([P, H], U32, name="gew0", align_bytes=64),
            sb.tile([P, H], U32, name="gew1", align_bytes=64),
        ]
        for h in range(S // H):
            nc.vector.tensor_copy(gew[h][:], ew[:].indirect(radar_t[:, h * H // 16 : (h + 1) * H // 16]))

        for c0, w in CHUNKS:
            cols = slice(c0, c0 + w)
            bank = ps.tile([P, 2, w], F32, name="ps_e%d" % c0)
            for i in range(2):
                product(bank[:, i, :], w1, i, gew[c0 // H][:, c0 % H : c0 % H + w], ges[:, cols])
            rect = sb.tile([P, 2, w], F32, name="rect_e%d" % c0)
            nc.scalar.activation(rect[:], bank[:], ACT.Relu)
            prod = sb.tile([P, 2, w], F32, name="prod%d" % c0)
            nc.vector.scalar_tensor_tensor(prod[:], rect[:], 2.0, plus2[:, :, cols], ALU.add, ALU.mult)
            den = sb.tile([P, w], F32, name="den%d" % c0)
            nc.vector.tensor_tensor(den[:], prod[:, 0, :], prod[:, 1, :], ALU.add)
            root = sb.tile([P, w], F32, name="root%d" % c0)
            nc.scalar.activation(root[:], den[:], ACT.Abs_reciprocal_sqrt, bias=-4.0)
            inv = sb.tile([P, w], F32, name="inv%d" % c0)
            nc.scalar.activation(inv[:], root[:], ACT.Square)
            res = sb.tile([P, w], F32, name="res%d" % c0)
            if c0 < 256:
                share = sb.tile([P, w], F32, name="share%d" % c0)
                nc.vector.scalar_tensor_tensor(share[:], prod[:, 1, :], -2.0, inv[:], ALU.add, ALU.mult)
                nc.scalar.activation(res[:], share[:], ACT.Identity, bias=1.0, scale=-2.0)
            else:
                num = sb.tile([P, w], F32, name="num%d" % c0)
                nc.vector.tensor_tensor(num[:], prod[:, 0, :], prod[:, 1, :], ALU.subtract)
                nc.vector.tensor_tensor(res[:], num[:], inv[:], ALU.mult)
            nc.sync.dma_start(out[:, cols], res[:])
